import numpy as np
import ml_dtypes


def mxq(x, axis, fmt="e4m3"):
    dtype, down = {"e4m3": (ml_dtypes.float8_e4m3fn, 7), "e5m2": (ml_dtypes.float8_e5m2, 14)}[fmt]
    v = np.moveaxis(np.asarray(x, np.float32).astype(ml_dtypes.bfloat16).astype(np.float64), axis, -1)
    blocks = v.reshape(v.shape[:-1] + (-1, 32))
    amax = np.abs(blocks).max(-1, keepdims=True)
    byte = np.maximum(np.where(amax > 0, np.frexp(amax)[1] - 1 + 127, 0) - down, 1)
    scale = np.exp2(byte - 127.0)
    codes = (blocks / scale).astype(np.float32).astype(dtype).astype(np.float64)
    return np.moveaxis((codes * scale).reshape(v.shape), -1, axis)


WIDE = False


def mx_kscale(k):
    if not WIDE:
        return np.ones(k)
    levels = np.array([10, -10, 5, -5, 0])
    if k % 512:
        return np.exp2(np.random.permutation(np.resize(levels, k // 32))).repeat(32)
    a = np.empty((k // 512, 16))
    for p in range(k // 512):
        a[p, :8] = np.random.permutation(np.resize(levels, 8))
        for g in range(8):
            far = levels[np.abs(levels - a[p, g]) >= 10]
            a[p, g + 8] = far[np.random.randint(len(far))]
    return np.exp2(a.ravel()).repeat(32)


def f64(x):
    return np.asarray(x).astype(np.float64)


def striped(idx):
    return np.tile(idx.reshape(-1, 16).T, (8, 1)).astype(np.uint16)


def unstriped(offs):
    return offs[:16].T.reshape(-1).astype(np.int64)


def striped8(idx):
    return np.concatenate([x.reshape(-1, 16).T for x in idx]).astype(np.uint16)


def runs(offs, k):
    lists = np.stack([offs[16 * r : 16 * r + 16].T.reshape(-1) for r in range(8)]).astype(np.int64)
    return lists[np.arange(k) % 512 // 64]


def pack_weight(w):
    k, n = w.shape
    w = f64(np.asarray(w, np.float32).astype(ml_dtypes.bfloat16)).reshape(k // 32, 32, n)
    amax = np.abs(w).max(1)
    byte = np.clip(np.where(amax > 0, np.frexp(amax)[1] - 1 + 127 - 7, 1), 1, 254)
    scaled = (w * np.exp2(127.0 - byte)[:, None, :]).reshape(k, n).astype(np.float32)
    words = np.ascontiguousarray(scaled.reshape(k // 512, 128, 4, n).transpose(0, 1, 3, 2)).astype(ml_dtypes.float8_e4m3fn).view(np.uint8)
    return words, np.ascontiguousarray(byte.astype(np.uint8).reshape(k // 512, 16, n))


def unpack_weight(words, scales):
    g, p, n, _ = words.shape
    vals = np.ascontiguousarray(words).view(ml_dtypes.float8_e4m3fn).astype(np.float64) * np.repeat(np.exp2(scales.astype(np.float64) - 127.0), 8, axis=1)[..., None]
    return vals.transpose(0, 1, 3, 2).reshape(g * 512, n)


K, T, S, N, H, W = 512, 2048, 512, 512, 512, 384


def setup_inputs():
    n = np.random.standard_normal
    s = mx_kscale(K)[:, None]
    u = mx_kscale(H)
    packed_xT = pack_weight(n((K, T)) * s)
    return {
        "x_words": packed_xT[0],
        "x_scales": packed_xT[1],
        "w1": (n((K, H)) / np.sqrt(K) / s).astype(np.float32),
        "gn": (np.random.uniform(0.5, 1.5, (H, 1)) * u[:, None]).astype(np.float32),
        "w2": (n((H, N)) / np.sqrt(2 * H) / u[:, None]).astype(np.float32),
        "w3": (n((K, N)) / np.sqrt(2 * K) / s).astype(np.float32),
        "offs": striped8(np.random.randint(0, T, (8, S))),
        "n1": striped(np.random.permutation(S)[:W]),
        "n2": striped(np.random.permutation(S)[:W]),
        "two": striped(np.random.permutation(T)[:S]),
        "n3": striped8(np.stack([np.random.permutation(S) for _ in range(8)])),
        "n4": striped8(np.stack([np.random.permutation(S) for _ in range(8)])),
    }


def reference(x_words, x_scales, w1, gn, w2, w3, offs, n1, n2, two, n3, n4):
    xq = unpack_weight(x_words, x_scales)[np.arange(K)[:, None], runs(offs, K)]
    y = mxq(f64(w1), 0, "e4m3").T @ xq
    old = y[:, unstriped(n1)]
    pa = y[:, unstriped(n2)]
    ra = old - np.tanh(pa)
    ds = y.copy()
    ds[:, unstriped(n1)] = ra
    z = f64(gn) * ds
    x_two = unpack_weight(x_words, x_scales)[:, unstriped(two)]
    h = mxq(f64(w2), 0, "e4m3").T @ mxq(z, 0, "e4m3") + mxq(f64(w3), 0, "e4m3").T @ x_two
    ex = np.exp(0.5 * h)
    return (2.0 * ex) / (ex + ex[np.arange(N)[:, None], runs(n3, N)] + ex[np.arange(N)[:, None], runs(n4, N)])

@@ -1,0 +1,213 @@
+from contextlib import ExitStack
+
+import concourse.mybir as mybir
+
+K, T, S, N, H, W = 512, 2048, 512, 512, 512, 384
+FLOPS = 2 * K * H * S + 2 * H * N * S + 2 * K * N * S
+
+F32 = mybir.dt.float32
+BF16 = mybir.dt.bfloat16
+I32 = mybir.dt.int32
+U32 = mybir.dt.uint32
+U16 = mybir.dt.uint16
+U8 = mybir.dt.uint8
+FP8X4 = mybir.dt.float8_e4m3fn_x4
+ACT = mybir.ActivationFunctionType
+ALU = mybir.AluOpType
+
+P = 128
+PACK = 4
+HALF = S // 2
+
+
+def deal(engine_copy, dealt, raw, first, count):
+    engine_copy(
+        out=dealt[:].rearrange("p (t m j) -> p m j t", t=PACK, j=PACK)[:, first : first + count],
+        in_=raw.rearrange("p j (m t) -> p m j t", t=PACK),
+    )
+
+
+def tile_picked_hmixktanhshare_none_p_kernel(tc, x_words, x_scales, w1, gn, w2, w3, offs, n1, n2, two, n3, n4, out):
+    nc = tc.nc
+    with ExitStack() as ctx:
+        keep = ctx.enter_context(tc.tile_pool(name="keep", bufs=1))
+        psum = ctx.enter_context(tc.psum_pool(name="psum", bufs=1))
+
+        def load_list(name, src):
+            tile = keep.tile([P, src.shape[1]], U16, name=name)
+            nc.sync.dma_start(out=tile[:], in_=src)
+            return tile
+
+        byte_table = keep.tile([P, T], U8, align_bytes=64)
+        nc.gpsimd.memset(byte_table[:].bitcast(I32), 0)
+        rows = x_scales[0].bitcast(I32)
+        nc.scalar.dma_start(out=byte_table[:].bitcast(I32)[0:P:8, :], in_=rows)
+
+        offs_sb = load_list("offs_sb", offs)
+        two_sb = load_list("two_sb", two)
+        n2_sb = load_list("n2_sb", n2)
+        n1_sb = load_list("n1_sb", n1)
+        word_table = keep.tile([P, T], U32, align_bytes=64)
+        nc.sync.dma_start(out=word_table[:].bitcast(I32), in_=x_words[0].rearrange("p n t -> p (n t)").bitcast(I32))
+
+        def load_weight(w):
+            halves = []
+            for half in range(2):
+                raw = keep.tile([P, PACK, H // 2], F32, name="raw%d" % half, tag="raw%d" % half)
+                nc.sync.dma_start(out=raw[:], in_=w.rearrange("(p j) c -> p j c", j=PACK)[:, :, half * (H // 2) : (half + 1) * (H // 2)])
+                halves.append(raw)
+            return halves
+
+        def place_scales(name, picked):
+            plane = keep.tile([P, S], U8, align_bytes=64, name=name)
+            nc.vector.tensor_copy(out=plane[:].bitcast(I32), in_=picked[:].bitcast(I32))
+            for r in range(1, 4):
+                nc.sync.dma_start(out=plane[:].bitcast(I32)[r:P:32, :], in_=picked[:].bitcast(I32)[8 * r : P : 32, :])
+            return plane
+
+        w1_raw = load_weight(w1)
+        n3_sb = load_list("n3_sb", n3)
+        n4_sb = load_list("n4_sb", n4)
+
+        picked_bytes = keep.tile([P, S], U8, align_bytes=64)
+        nc.vector.tensor_copy(out=picked_bytes[:], in_=byte_table[:].indirect(offs_sb[:]))
+        xq_scales = place_scales("xq_scales", picked_bytes)
+        xq_words = keep.tile([P, S], U32, align_bytes=64)
+        nc.vector.tensor_copy(out=xq_words[:], in_=word_table[:].indirect(offs_sb[:]))
+        two_words = keep.tile([P, S], U32, align_bytes=64)
+        nc.vector.tensor_copy(out=two_words[:], in_=word_table[:].indirect(two_sb[:]))
+
+        w1_bf = keep.tile([P, PACK * H], BF16, align_bytes=64, tag="w1_bf")
+        deal(nc.scalar.copy, w1_bf, w1_raw[0][:], 0, 64)
+        deal(nc.scalar.copy, w1_bf, w1_raw[1][:], 64, 64)
+        w1_codes = keep.tile([P, H], U32, align_bytes=64)
+        w1_scales = keep.tile([P, H], U8, align_bytes=64)
+        y_banks = []
+        for t in range(PACK):
+            cols = slice(t * P, (t + 1) * P)
+            nc.vector.quantize_mx(out=w1_codes[:, cols].bitcast(FP8X4), scales=w1_scales[:, cols], in_=w1_bf[:, t * PACK * P : (t + 1) * PACK * P])
+        for t in range(PACK):
+            cols = slice(t * P, (t + 1) * P)
+            bank = psum.tile([P, S], F32, name="y_bank%d" % t)
+            nc.tensor.matmul_mx(out=bank[:], lhsT=w1_codes[:, cols].bitcast(FP8X4), lhsT_scale=w1_scales[:, cols],
+                                rhs=xq_words[:].bitcast(FP8X4), rhs_scale=xq_scales[:], start=True, stop=True)
+            y_banks.append(bank)
+
+        two_bytes = keep.tile([P, S], U8, align_bytes=64)
+        nc.vector.tensor_copy(out=two_bytes[:], in_=byte_table[:].indirect(two_sb[:]))
+        two_scales = place_scales("two_scales", two_bytes)
+        gain = keep.tile([P, PACK], F32)
+        nc.gpsimd.dma_start(out=gain[:], in_=gn.rearrange("(p t) o -> p (t o)", t=PACK))
+
+        w3_raw = load_weight(w3)
+        w3_bf = keep.tile([P, PACK * N], BF16, align_bytes=64)
+        for half in range(2):
+            deal(nc.vector.tensor_copy, w3_bf, w3_raw[half][:], half * 64, 64)
+        w2_raw = keep.tile([P, PACK, N], F32, align_bytes=64, name="w2_raw", tag="w1_bf")
+        nc.sync.dma_start(out=w2_raw[:], in_=w2.rearrange("(p j) c -> p j c", j=PACK))
+        w3_codes = keep.tile([P, N], U32, align_bytes=64)
+        w3_scales = keep.tile([P, N], U8, align_bytes=64)
+
+        z_planes = keep.tile([P, PACK, S], BF16, align_bytes=64)
+        for t in range(PACK):
+            y_sb = keep.tile([P, S], F32, name="y_sb%d" % t)
+            nc.scalar.copy(out=y_sb[:], in_=y_banks[t][:])
+            pa = keep.tile([P, W], F32, name="pa%d" % t, tag="pa%d" % t, align_bytes=64)
+            nc.scalar.activation(out=pa[:], in_=y_sb[:].indirect(n2_sb[:]), func=ACT.Copy)
+            minus_tanh = keep.tile([P, W], F32, name="minus_tanh%d" % t)
+            old = keep.tile([P, W], F32, name="old%d" % t)
+            nc.scalar.activation(out=old[:], in_=y_sb[:].indirect(n1_sb[:]), func=ACT.Copy)
+            nc.scalar.activation(out=minus_tanh[:], in_=pa[:], func=ACT.Tanh, scale=-1.0)
+            if t == 0:
+                nc.vector.quantize_mx(out=w3_codes[:].bitcast(FP8X4), scales=w3_scales[:], in_=w3_bf[:])
+            for half in range(2):
+                entries = slice(half * (W // 2), (half + 1) * (W // 2))
+                nc.vector.tensor_tensor(out=y_sb[:].indirect(n1_sb[:, half * (W // 32) : (half + 1) * (W // 32)]),
+                                        in0=old[:, entries], in1=minus_tanh[:, entries], op=ALU.add)
+            for cols in [slice(0, S)] if t < PACK - 1 else [slice(HALF, S), slice(0, HALF)]:
+                nc.vector.tensor_scalar(out=z_planes[:, t, cols], in0=y_sb[:, cols], scalar1=gain[:, t : t + 1], scalar2=None, op0=ALU.mult)
+
+        w2_bf = keep.tile([P, PACK * N], BF16, align_bytes=64, name="w2_bf", tag="pa3")
+        deal(nc.scalar.copy, w2_bf, w2_raw[:], 0, P)
+        w2_codes = keep.tile([P, N], U32, align_bytes=64)
+        w2_scales = keep.tile([P, N], U8, align_bytes=64)
+
+        z_bf = keep.tile([P, S * PACK], BF16, align_bytes=64)
+        z_to = z_bf[:].rearrange("p (c i t) -> p c t i", i=4, t=PACK)
+        z_from = z_planes[:].rearrange("p t (c i) -> p c t i", i=4)
+        nc.scalar.copy(out=z_to[:, 80:128], in_=z_from[:, 80:128])
+        nc.vector.tensor_copy(out=z_to[:, 0:64], in_=z_from[:, 0:64])
+        nc.vector.tensor_copy(out=z_to[:, 64:80], in_=z_from[:, 64:80])
+        z_codes = keep.tile([P, S], U32, align_bytes=64)
+        z_scales = keep.tile([P, S], U8, align_bytes=64)
+
+        def quantize_z(half):
+            cols = slice(half * HALF, (half + 1) * HALF)
+            nc.vector.quantize_mx(out=z_codes[:, cols].bitcast(FP8X4), scales=z_scales[:, cols],
+                                  in_=z_bf[:, half * HALF * PACK : (half + 1) * HALF * PACK])
+
+        def quantize_w2(t):
+            cols = slice(t * P, (t + 1) * P)
+            nc.vector.quantize_mx(out=w2_codes[:, cols].bitcast(FP8X4), scales=w2_scales[:, cols], in_=w2_bf[:, t * PACK * P : (t + 1) * PACK * P])
+
+        quantize_z(0)
+        quantize_w2(0)
+        quantize_z(1)
+        for t in range(1, PACK):
+            quantize_w2(t)
+
+        h_banks = []
+        for t in range(PACK):
+            cols = slice(t * P, (t + 1) * P)
+            bank = psum.tile([P, S], F32, name="h_bank%d" % t)
+            nc.tensor.matmul_mx(out=bank[:], lhsT=w3_codes[:, cols].bitcast(FP8X4), lhsT_scale=w3_scales[:, cols],
+                                rhs=two_words[:].bitcast(FP8X4), rhs_scale=two_scales[:], start=True, stop=False)
+            h_banks.append(bank)
+        for t in range(PACK):
+            cols = slice(t * P, (t + 1) * P)
+            for half in range(2):
+                places = slice(half * HALF, (half + 1) * HALF)
+                nc.tensor.matmul_mx(out=h_banks[t][:, places], lhsT=w2_codes[:, cols].bitcast(FP8X4), lhsT_scale=w2_scales[:, cols],
+                                    rhs=z_codes[:, places].bitcast(FP8X4), rhs_scale=z_scales[:, places], start=False, stop=(half == 1))
+
+        ex, inv = [], []
+        for t in range(PACK):
+            ex_t = keep.tile([P, S], F32, name="ex%d" % t)
+            nc.scalar.activation(out=ex_t[:], in_=h_banks[t][:], func=ACT.Exp, scale=0.5)
+            ex.append(ex_t)
+        for t in range(PACK):
+            inv_t = keep.tile([P, S], F32, name="inv%d" % t)
+            nc.scalar.activation(out=inv_t[:], in_=h_banks[t][:], func=ACT.Exp, scale=-0.5)
+            inv.append(inv_t)
+        out_rows = out.rearrange("(p t) n -> t p n", t=PACK)
+        at_n3 = [keep.tile([P, S], F32, name="at_n3_%d" % t) for t in range(PACK)]
+        for t in range(2, PACK):
+            for half in range(2):
+                nc.scalar.activation(out=at_n3[t][:, half * HALF : (half + 1) * HALF],
+                                     in_=ex[t][:].indirect(n3_sb[:, half * 16 : (half + 1) * 16]), func=ACT.Copy)
+        ratios = []
+        for t in range(PACK):
+            both = keep.tile([P, S], F32, name="both%d" % t)
+            ratio = keep.tile([P, S], F32, name="ratio%d" % t)
+            if t < 2:
+                for half in range(2):
+                    nc.vector.tensor_copy(out=at_n3[t][:, half * HALF : (half + 1) * HALF],
+                                          in_=ex[t][:].indirect(n3_sb[:, half * 16 : (half + 1) * 16]))
+            for half in range(2):
+                cols = slice(half * HALF, (half + 1) * HALF)
+                nc.vector.tensor_tensor(out=both[:, cols], in0=ex[t][:].indirect(n4_sb[:, half * 16 : (half + 1) * 16]),
+                                        in1=at_n3[t][:, cols], op=ALU.add)
+            for half in range(2):
+                cols = slice(half * HALF, (half + 1) * HALF)
+                nc.vector.tensor_tensor(out=ratio[:, cols], in0=both[:, cols], in1=inv[t][:, cols], op=ALU.mult)
+            ratios.append(ratio)
+        for t in range(PACK):
+            root = keep.tile([P, S], F32, name="root%d" % t)
+            result = keep.tile([P, S], F32, name="result%d" % t)
+            for half in range(2):
+                cols = slice(half * HALF, (half + 1) * HALF)
+                nc.scalar.activation(out=root[:, cols], in_=ratios[t][:, cols], func=ACT.Abs_reciprocal_sqrt, scale=0.5, bias=0.5)
+            for half in range(2):
+                cols = slice(half * HALF, (half + 1) * HALF)
+                nc.scalar.activation(out=result[:, cols], in_=root[:, cols], func=ACT.Square)
+                nc.sync.dma_start(out=out_rows[t][:, cols], in_=result[:, cols])

@@ -39,7 +39,7 @@ def tile_picked_hmixktanhshare_none_p_kernel(tc, x_words, x_scales, w1, gn, w2, 
             return tile
 
         byte_table = keep.tile([P, T], U8, align_bytes=64)
-        nc.gpsimd.memset(byte_table[:].bitcast(I32), 0)
+        nc.vector.memset(byte_table[:].bitcast(I32), 0)
         rows = x_scales[0].bitcast(I32)
         nc.scalar.dma_start(out=byte_table[:].bitcast(I32)[0:P:8, :], in_=rows)
 
@@ -93,44 +93,74 @@ def tile_picked_hmixktanhshare_none_p_kernel(tc, x_words, x_scales, w1, gn, w2, 
                                 rhs=xq_words[:].bitcast(FP8X4), rhs_scale=xq_scales[:], start=True, stop=True)
             y_banks.append(bank)
 
+        w3_raw = load_weight(w3)
         two_bytes = keep.tile([P, S], U8, align_bytes=64)
         nc.vector.tensor_copy(out=two_bytes[:], in_=byte_table[:].indirect(two_sb[:]))
-        two_scales = place_scales("two_scales", two_bytes)
         gain = keep.tile([P, PACK], F32)
         nc.gpsimd.dma_start(out=gain[:], in_=gn.rearrange("(p t) o -> p (t o)", t=PACK))
-
-        w3_raw = load_weight(w3)
-        w3_bf = keep.tile([P, PACK * N], BF16, align_bytes=64)
-        for half in range(2):
-            deal(nc.vector.tensor_copy, w3_bf, w3_raw[half][:], half * 64, 64)
         w2_raw = keep.tile([P, PACK, N], F32, align_bytes=64, name="w2_raw", tag="w1_bf")
         nc.sync.dma_start(out=w2_raw[:], in_=w2.rearrange("(p j) c -> p j c", j=PACK))
+        two_scales = place_scales("two_scales", two_bytes)
+
+        z_planes = keep.tile([P, PACK, S], BF16, align_bytes=64, tag="z_planes")
+        y_sb = [keep.tile([P, S if t == 2 else 2 * W], F32, name="y_sb%d" % t) for t in range(PACK)]
+        pa = [keep.tile([P, W], F32, name="pa%d" % t, tag="pa%d" % t, align_bytes=64) for t in range(PACK)]
+        minus_tanh = [keep.tile([P, W], F32, name="minus_tanh%d" % t) for t in range(PACK)]
+        old = [keep.tile([P, W], F32, name="old%d" % t) for t in range(PACK)]
+        ex = [keep.tile([P, 2 * S], F32, name="ex%d" % t) for t in range(PACK)]
+        for t in (0, 1, 3):
+            nc.gpsimd.memset(y_sb[t][:, S:], 0.0)
+        for t in range(PACK):
+            nc.gpsimd.memset(ex[t][:, S:], 0.0)
+
+        def fetch_tanh(t):
+            nc.scalar.activation(out=pa[t][:], in_=y_sb[t][:].indirect(n2_sb[:]), func=ACT.Copy)
+            nc.scalar.activation(out=minus_tanh[t][:], in_=pa[t][:], func=ACT.Tanh, scale=-1.0)
+
+        def scatter_sum(t):
+            nc.vector.tensor_tensor(out=y_sb[t][:].indirect(n1_sb[:]), in0=old[t][:], in1=minus_tanh[t][:], op=ALU.add)
+
+        def gain_plane(t, cols):
+            nc.vector.tensor_scalar(out=z_planes[:, t, cols], in0=y_sb[t][:, cols], scalar1=gain[:, t : t + 1], scalar2=None, op0=ALU.mult)
+
+        w3_bf = keep.tile([P, PACK * N], BF16, align_bytes=64)
+        w2_bf = keep.tile([P, PACK * N], BF16, align_bytes=64)
+        nc.scalar.copy(out=y_sb[0][:, :S], in_=y_banks[0][:])
+        nc.vector.tensor_copy(out=y_sb[1][:, :S], in_=y_banks[1][:])
+        fetch_tanh(0)
+        nc.vector.tensor_copy(out=old[0][:], in_=y_sb[0][:].indirect(n1_sb[:]))
+        scatter_sum(0)
+        fetch_tanh(1)
+        nc.scalar.activation(out=old[1][:], in_=y_sb[1][:].indirect(n1_sb[:]), func=ACT.Copy)
+        for half in range(2):
+            deal(nc.vector.tensor_copy, w3_bf, w3_raw[half][:], half * 64, 64)
+        gain_plane(0, slice(0, S))
+        scatter_sum(1)
+        nc.scalar.copy(out=y_sb[2][:, :S], in_=y_banks[2][:])
+        fetch_tanh(2)
+        nc.scalar.copy(out=y_sb[3][:, :S], in_=y_banks[3][:])
+        fetch_tanh(3)
+        nc.vector.tensor_tensor(out=old[2][:], in0=y_sb[2][:].indirect(n1_sb[:]), in1=minus_tanh[2][:], op=ALU.add)
+        gain_plane(1, slice(0, S))
+        nc.scalar.activation(out=old[3][:], in_=y_sb[3][:].indirect(n1_sb[:]), func=ACT.Copy)
+        deal(nc.scalar.copy, w2_bf, w2_raw[:], 0, P)
+        scatter_sum(3)
+        nc.scalar.activation(out=y_sb[2][:].indirect(n1_sb[:]), in_=old[2][:], func=ACT.Copy)
+        gain_plane(3, slice(0, S))
+        nc.scalar.activation(out=z_planes[:, 2, 320:S], in_=y_sb[2][:, 320:S], func=ACT.Copy, scale=gain[:, 2:3])
+        gain_plane(2, slice(0, 320))
+
         w3_codes = keep.tile([P, N], U32, align_bytes=64)
         w3_scales = keep.tile([P, N], U8, align_bytes=64)
-
-        z_planes = keep.tile([P, PACK, S], BF16, align_bytes=64)
-        for t in range(PACK):
-            y_sb = keep.tile([P, S], F32, name="y_sb%d" % t)
-            nc.scalar.copy(out=y_sb[:], in_=y_banks[t][:])
-            pa = keep.tile([P, W], F32, name="pa%d" % t, tag="pa%d" % t, align_bytes=64)
-            nc.scalar.activation(out=pa[:], in_=y_sb[:].indirect(n2_sb[:]), func=ACT.Copy)
-            minus_tanh = keep.tile([P, W], F32, name="minus_tanh%d" % t)
-            old = keep.tile([P, W], F32, name="old%d" % t)
-            nc.scalar.activation(out=old[:], in_=y_sb[:].indirect(n1_sb[:]), func=ACT.Copy)
-            nc.scalar.activation(out=minus_tanh[:], in_=pa[:], func=ACT.Tanh, scale=-1.0)
-            if t == 0:
-                nc.vector.quantize_mx(out=w3_codes[:].bitcast(FP8X4), scales=w3_scales[:], in_=w3_bf[:])
-            for half in range(2):
-                entries = slice(half * (W // 2), (half + 1) * (W // 2))
-                nc.vector.tensor_tensor(out=y_sb[:].indirect(n1_sb[:, half * (W // 32) : (half + 1) * (W // 32)]),
-                                        in0=old[:, entries], in1=minus_tanh[:, entries], op=ALU.add)
-            for cols in [slice(0, S)] if t < PACK - 1 else [slice(HALF, S), slice(0, HALF)]:
-                nc.vector.tensor_scalar(out=z_planes[:, t, cols], in0=y_sb[:, cols], scalar1=gain[:, t : t + 1], scalar2=None, op0=ALU.mult)
-
-        w2_bf = keep.tile([P, PACK * N], BF16, align_bytes=64, name="w2_bf", tag="pa3")
-        deal(nc.scalar.copy, w2_bf, w2_raw[:], 0, P)
-        w2_codes = keep.tile([P, N], U32, align_bytes=64)
+        nc.vector.quantize_mx(out=w3_codes[:].bitcast(FP8X4), scales=w3_scales[:], in_=w3_bf[:])
+        first_codes = keep.tile([P, P], U32, align_bytes=64)
         w2_scales = keep.tile([P, N], U8, align_bytes=64)
+
+        def quantize_w2(t, codes):
+            nc.vector.quantize_mx(out=codes.bitcast(FP8X4), scales=w2_scales[:, t * P : (t + 1) * P],
+                                  in_=w2_bf[:, t * PACK * P : (t + 1) * PACK * P])
+
+        quantize_w2(0, first_codes[:])
 
         z_bf = keep.tile([P, S * PACK], BF16, align_bytes=64)
         z_to = z_bf[:].rearrange("p (c i t) -> p c t i", i=4, t=PACK)
@@ -146,15 +176,11 @@ def tile_picked_hmixktanhshare_none_p_kernel(tc, x_words, x_scales, w1, gn, w2, 
             nc.vector.quantize_mx(out=z_codes[:, cols].bitcast(FP8X4), scales=z_scales[:, cols],
                                   in_=z_bf[:, half * HALF * PACK : (half + 1) * HALF * PACK])
 
-        def quantize_w2(t):
-            cols = slice(t * P, (t + 1) * P)
-            nc.vector.quantize_mx(out=w2_codes[:, cols].bitcast(FP8X4), scales=w2_scales[:, cols], in_=w2_bf[:, t * PACK * P : (t + 1) * PACK * P])
-
         quantize_z(0)
-        quantize_w2(0)
         quantize_z(1)
+        later_codes = keep.tile([P, PACK - 1, P], U32, align_bytes=64, tag="z_planes")
         for t in range(1, PACK):
-            quantize_w2(t)
+            quantize_w2(t, later_codes[:, t - 1, :])
 
         h_banks = []
         for t in range(PACK):
@@ -165,49 +191,37 @@ def tile_picked_hmixktanhshare_none_p_kernel(tc, x_words, x_scales, w1, gn, w2, 
             h_banks.append(bank)
         for t in range(PACK):
             cols = slice(t * P, (t + 1) * P)
-            for half in range(2):
-                places = slice(half * HALF, (half + 1) * HALF)
-                nc.tensor.matmul_mx(out=h_banks[t][:, places], lhsT=w2_codes[:, cols].bitcast(FP8X4), lhsT_scale=w2_scales[:, cols],
-                                    rhs=z_codes[:, places].bitcast(FP8X4), rhs_scale=z_scales[:, places], start=False, stop=(half == 1))
+            codes = first_codes[:] if t == 0 else later_codes[:, t - 1, :]
+            for places in [slice(0, HALF), slice(HALF, S)] if t == 0 else [slice(0, S)]:
+                nc.tensor.matmul_mx(out=h_banks[t][:, places], lhsT=codes.bitcast(FP8X4), lhsT_scale=w2_scales[:, cols],
+                                    rhs=z_codes[:, places].bitcast(FP8X4), rhs_scale=z_scales[:, places], start=False, stop=(places.stop == S))
 
-        ex, inv = [], []
-        for t in range(PACK):
-            ex_t = keep.tile([P, S], F32, name="ex%d" % t)
-            nc.scalar.activation(out=ex_t[:], in_=h_banks[t][:], func=ACT.Exp, scale=0.5)
-            ex.append(ex_t)
-        for t in range(PACK):
-            inv_t = keep.tile([P, S], F32, name="inv%d" % t)
-            nc.scalar.activation(out=inv_t[:], in_=h_banks[t][:], func=ACT.Exp, scale=-0.5)
-            inv.append(inv_t)
         out_rows = out.rearrange("(p t) n -> t p n", t=PACK)
+        inv = [keep.tile([P, S], F32, name="inv%d" % t) for t in range(PACK)]
         at_n3 = [keep.tile([P, S], F32, name="at_n3_%d" % t) for t in range(PACK)]
+        ratios = [keep.tile([P, S], F32, name="ratio%d" % t) for t in range(PACK)]
+        pieces = [[slice(0, S)]] * (PACK - 1) + [[slice(0, HALF), slice(HALF, S)]]
+        for t in range(PACK):
+            nc.scalar.activation(out=ex[t][:, :S], in_=h_banks[t][:], func=ACT.Exp, scale=0.5)
+            nc.scalar.activation(out=inv[t][:], in_=h_banks[t][:], func=ACT.Exp, scale=-0.5)
         for t in range(2, PACK):
-            for half in range(2):
-                nc.scalar.activation(out=at_n3[t][:, half * HALF : (half + 1) * HALF],
-                                     in_=ex[t][:].indirect(n3_sb[:, half * 16 : (half + 1) * 16]), func=ACT.Copy)
-        ratios = []
+            nc.scalar.activation(out=at_n3[t][:], in_=ex[t][:].indirect(n3_sb[:]), func=ACT.Copy)
         for t in range(PACK):
             both = keep.tile([P, S], F32, name="both%d" % t)
-            ratio = keep.tile([P, S], F32, name="ratio%d" % t)
             if t < 2:
-                for half in range(2):
-                    nc.vector.tensor_copy(out=at_n3[t][:, half * HALF : (half + 1) * HALF],
-                                          in_=ex[t][:].indirect(n3_sb[:, half * 16 : (half + 1) * 16]))
-            for half in range(2):
-                cols = slice(half * HALF, (half + 1) * HALF)
-                nc.vector.tensor_tensor(out=both[:, cols], in0=ex[t][:].indirect(n4_sb[:, half * 16 : (half + 1) * 16]),
+                nc.vector.tensor_copy(out=at_n3[t][:], in_=ex[t][:].indirect(n3_sb[:]))
+            for cols in pieces[t]:
+                nc.vector.tensor_tensor(out=both[:, cols], in0=ex[t][:].indirect(n4_sb[:, cols.start // 16 : cols.stop // 16]),
                                         in1=at_n3[t][:, cols], op=ALU.add)
-            for half in range(2):
-                cols = slice(half * HALF, (half + 1) * HALF)
-                nc.vector.tensor_tensor(out=ratio[:, cols], in0=both[:, cols], in1=inv[t][:, cols], op=ALU.mult)
-            ratios.append(ratio)
+            for cols in pieces[t]:
+                nc.vector.tensor_tensor(out=ratios[t][:, cols], in0=both[:, cols], in1=inv[t][:, cols], op=ALU.mult)
         for t in range(PACK):
             root = keep.tile([P, S], F32, name="root%d" % t)
             result = keep.tile([P, S], F32, name="result%d" % t)
-            for half in range(2):
-                cols = slice(half * HALF, (half + 1) * HALF)
+            for cols in pieces[t]:
                 nc.scalar.activation(out=root[:, cols], in_=ratios[t][:, cols], func=ACT.Abs_reciprocal_sqrt, scale=0.5, bias=0.5)
-            for half in range(2):
-                cols = slice(half * HALF, (half + 1) * HALF)
-                nc.scalar.activation(out=result[:, cols], in_=root[:, cols], func=ACT.Square)
+                if t < PACK - 1:
+                    nc.scalar.activation(out=result[:, cols], in_=root[:, cols], func=ACT.Square)
+                else:
+                    nc.vector.tensor_tensor(out=result[:, cols], in0=root[:, cols], in1=root[:, cols], op=ALU.mult)
                 nc.sync.dma_start(out=out_rows[t][:, cols], in_=result[:, cols])

@@ -39,14 +39,11 @@ def tile_picked_hmixktanhshare_none_p_kernel(tc, x_words, x_scales, w1, gn, w2, 
             return tile
 
         byte_table = keep.tile([P, T], U8, align_bytes=64)
-        nc.vector.memset(byte_table[:].bitcast(I32), 0)
         rows = x_scales[0].bitcast(I32)
-        nc.scalar.dma_start(out=byte_table[:].bitcast(I32)[0:P:8, :], in_=rows)
 
         offs_sb = load_list("offs_sb", offs)
+        nc.sync.dma_start(out=byte_table[:].bitcast(I32), in_=rows.unsqueeze(1).to_broadcast([16, 8, T // 4]))
         two_sb = load_list("two_sb", two)
-        n2_sb = load_list("n2_sb", n2)
-        n1_sb = load_list("n1_sb", n1)
         word_table = keep.tile([P, T], U32, align_bytes=64)
         nc.sync.dma_start(out=word_table[:].bitcast(I32), in_=x_words[0].rearrange("p n t -> p (n t)").bitcast(I32))
 
@@ -58,20 +55,22 @@ def tile_picked_hmixktanhshare_none_p_kernel(tc, x_words, x_scales, w1, gn, w2, 
                 halves.append(raw)
             return halves
 
-        def place_scales(name, picked):
+        def place_scales(name, picked, queue):
             plane = keep.tile([P, S], U8, align_bytes=64, name=name)
             nc.vector.tensor_copy(out=plane[:].bitcast(I32), in_=picked[:].bitcast(I32))
             for r in range(1, 4):
-                nc.sync.dma_start(out=plane[:].bitcast(I32)[r:P:32, :], in_=picked[:].bitcast(I32)[8 * r : P : 32, :])
+                queue.dma_start(out=plane[:].bitcast(I32)[r:P:32, :], in_=picked[:].bitcast(I32)[8 * r : P : 32, :])
             return plane
 
         w1_raw = load_weight(w1)
+        n2_sb = load_list("n2_sb", n2)
+        n1_sb = load_list("n1_sb", n1)
         n3_sb = load_list("n3_sb", n3)
         n4_sb = load_list("n4_sb", n4)
 
         picked_bytes = keep.tile([P, S], U8, align_bytes=64)
         nc.vector.tensor_copy(out=picked_bytes[:], in_=byte_table[:].indirect(offs_sb[:]))
-        xq_scales = place_scales("xq_scales", picked_bytes)
+        xq_scales = place_scales("xq_scales", picked_bytes, nc.sync)
         xq_words = keep.tile([P, S], U32, align_bytes=64)
         nc.vector.tensor_copy(out=xq_words[:], in_=word_table[:].indirect(offs_sb[:]))
         two_words = keep.tile([P, S], U32, align_bytes=64)
@@ -100,22 +99,27 @@ def tile_picked_hmixktanhshare_none_p_kernel(tc, x_words, x_scales, w1, gn, w2, 
         nc.gpsimd.dma_start(out=gain[:], in_=gn.rearrange("(p t) o -> p (t o)", t=PACK))
         w2_raw = keep.tile([P, PACK, N], F32, align_bytes=64, name="w2_raw", tag="w1_bf")
         nc.sync.dma_start(out=w2_raw[:], in_=w2.rearrange("(p j) c -> p j c", j=PACK))
-        two_scales = place_scales("two_scales", two_bytes)
+        two_scales = place_scales("two_scales", two_bytes, nc.gpsimd)
 
         z_planes = keep.tile([P, PACK, S], BF16, align_bytes=64, tag="z_planes")
         y_sb = [keep.tile([P, S if t == 2 else 2 * W], F32, name="y_sb%d" % t) for t in range(PACK)]
         pa = [keep.tile([P, W], F32, name="pa%d" % t, tag="pa%d" % t, align_bytes=64) for t in range(PACK)]
         minus_tanh = [keep.tile([P, W], F32, name="minus_tanh%d" % t) for t in range(PACK)]
-        old = [keep.tile([P, W], F32, name="old%d" % t) for t in range(PACK)]
-        ex = [keep.tile([P, 2 * S], F32, name="ex%d" % t) for t in range(PACK)]
+        old = [keep.tile([P, W], F32, name="old%d" % t, tag="old%d" % t, align_bytes=64) for t in range(PACK)]
         for t in (0, 1, 3):
             nc.gpsimd.memset(y_sb[t][:, S:], 0.0)
-        for t in range(PACK):
-            nc.gpsimd.memset(ex[t][:, S:], 0.0)
 
-        def fetch_tanh(t):
+        def leave_bank(t):
+            nc.scalar.copy(out=y_sb[t][:, :S], in_=y_banks[t][:])
+
+        def fetch_pa(t):
             nc.scalar.activation(out=pa[t][:], in_=y_sb[t][:].indirect(n2_sb[:]), func=ACT.Copy)
+
+        def tanh_pa(t):
             nc.scalar.activation(out=minus_tanh[t][:], in_=pa[t][:], func=ACT.Tanh, scale=-1.0)
+
+        def fetch_old(t):
+            nc.scalar.activation(out=old[t][:], in_=y_sb[t][:].indirect(n1_sb[:]), func=ACT.Copy)
 
         def scatter_sum(t):
             nc.vector.tensor_tensor(out=y_sb[t][:].indirect(n1_sb[:]), in0=old[t][:], in1=minus_tanh[t][:], op=ALU.add)
@@ -123,44 +127,48 @@ def tile_picked_hmixktanhshare_none_p_kernel(tc, x_words, x_scales, w1, gn, w2, 
         def gain_plane(t, cols):
             nc.vector.tensor_scalar(out=z_planes[:, t, cols], in0=y_sb[t][:, cols], scalar1=gain[:, t : t + 1], scalar2=None, op0=ALU.mult)
 
-        w3_bf = keep.tile([P, PACK * N], BF16, align_bytes=64)
-        w2_bf = keep.tile([P, PACK * N], BF16, align_bytes=64)
-        nc.scalar.copy(out=y_sb[0][:, :S], in_=y_banks[0][:])
-        nc.vector.tensor_copy(out=y_sb[1][:, :S], in_=y_banks[1][:])
-        fetch_tanh(0)
-        nc.vector.tensor_copy(out=old[0][:], in_=y_sb[0][:].indirect(n1_sb[:]))
-        scatter_sum(0)
-        fetch_tanh(1)
-        nc.scalar.activation(out=old[1][:], in_=y_sb[1][:].indirect(n1_sb[:]), func=ACT.Copy)
-        for half in range(2):
-            deal(nc.vector.tensor_copy, w3_bf, w3_raw[half][:], half * 64, 64)
-        gain_plane(0, slice(0, S))
-        scatter_sum(1)
-        nc.scalar.copy(out=y_sb[2][:, :S], in_=y_banks[2][:])
-        fetch_tanh(2)
-        nc.scalar.copy(out=y_sb[3][:, :S], in_=y_banks[3][:])
-        fetch_tanh(3)
-        nc.vector.tensor_tensor(out=old[2][:], in0=y_sb[2][:].indirect(n1_sb[:]), in1=minus_tanh[2][:], op=ALU.add)
-        gain_plane(1, slice(0, S))
-        nc.scalar.activation(out=old[3][:], in_=y_sb[3][:].indirect(n1_sb[:]), func=ACT.Copy)
-        deal(nc.scalar.copy, w2_bf, w2_raw[:], 0, P)
-        scatter_sum(3)
-        nc.scalar.activation(out=y_sb[2][:].indirect(n1_sb[:]), in_=old[2][:], func=ACT.Copy)
-        gain_plane(3, slice(0, S))
-        nc.scalar.activation(out=z_planes[:, 2, 320:S], in_=y_sb[2][:, 320:S], func=ACT.Copy, scale=gain[:, 2:3])
-        gain_plane(2, slice(0, 320))
-
         w3_codes = keep.tile([P, N], U32, align_bytes=64)
         w3_scales = keep.tile([P, N], U8, align_bytes=64)
-        nc.vector.quantize_mx(out=w3_codes[:].bitcast(FP8X4), scales=w3_scales[:], in_=w3_bf[:])
         first_codes = keep.tile([P, P], U32, align_bytes=64)
         w2_scales = keep.tile([P, N], U8, align_bytes=64)
+
+        leave_bank(0)
+        nc.vector.tensor_copy(out=y_sb[1][:, :S], in_=y_banks[1][:])
+        fetch_pa(0)
+        tanh_pa(0)
+        nc.vector.tensor_copy(out=old[0][:], in_=y_sb[0][:].indirect(n1_sb[:]))
+        scatter_sum(0)
+        fetch_pa(1)
+        leave_bank(2)
+        tanh_pa(1)
+        fetch_old(1)
+        w3_bf = keep.tile([P, PACK * N], BF16, align_bytes=64, name="w3_bf", tag="pa0")
+        deal(nc.vector.tensor_copy, w3_bf, w3_raw[0][:], 0, 64)
+        gain_plane(0, slice(0, S))
+        deal(nc.vector.tensor_copy, w3_bf, w3_raw[1][:], 64, 64)
+        scatter_sum(1)
+        nc.vector.quantize_mx(out=w3_codes[:].bitcast(FP8X4), scales=w3_scales[:], in_=w3_bf[:])
+        fetch_pa(2)
+        leave_bank(3)
+        tanh_pa(2)
+        fetch_pa(3)
+        fetch_old(3)
+        tanh_pa(3)
+        nc.vector.tensor_tensor(out=old[2][:], in0=y_sb[2][:].indirect(n1_sb[:]), in1=minus_tanh[2][:], op=ALU.add)
+        gain_plane(1, slice(0, S))
+        w2_bf = keep.tile([P, PACK * N], BF16, align_bytes=64, name="w2_bf", tag="pa2")
+        deal(nc.scalar.copy, w2_bf, w2_raw[:, :, 0:384], 0, 96)
+        deal(nc.vector.tensor_copy, w2_bf, w2_raw[:, :, 384:N], 96, 32)
+        scatter_sum(3)
+        nc.scalar.activation(out=y_sb[2][:].indirect(n1_sb[:]), in_=old[2][:], func=ACT.Copy)
 
         def quantize_w2(t, codes):
             nc.vector.quantize_mx(out=codes.bitcast(FP8X4), scales=w2_scales[:, t * P : (t + 1) * P],
                                   in_=w2_bf[:, t * PACK * P : (t + 1) * PACK * P])
 
         quantize_w2(0, first_codes[:])
+        gain_plane(3, slice(0, S))
+        nc.scalar.activation(out=z_planes[:, 2, :], in_=y_sb[2][:], func=ACT.Copy, scale=gain[:, 2:3])
 
         z_bf = keep.tile([P, S * PACK], BF16, align_bytes=64)
         z_to = z_bf[:].rearrange("p (c i t) -> p c t i", i=4, t=PACK)
@@ -197,31 +205,73 @@ def tile_picked_hmixktanhshare_none_p_kernel(tc, x_words, x_scales, w1, gn, w2, 
                                     rhs=z_codes[:, places].bitcast(FP8X4), rhs_scale=z_scales[:, places], start=False, stop=(places.stop == S))
 
         out_rows = out.rearrange("(p t) n -> t p n", t=PACK)
-        inv = [keep.tile([P, S], F32, name="inv%d" % t) for t in range(PACK)]
+        halves = [slice(0, HALF), slice(HALF, S)]
+        ex = [keep.tile([P, S if t == 0 else 2 * S], F32, name="ex%d" % t) for t in range(PACK)]
+        inv0 = keep.tile([P, S], F32)
+        inv = [inv0[:]] + [ex[t][:, S:] for t in range(1, PACK)]
         at_n3 = [keep.tile([P, S], F32, name="at_n3_%d" % t) for t in range(PACK)]
-        ratios = [keep.tile([P, S], F32, name="ratio%d" % t) for t in range(PACK)]
-        pieces = [[slice(0, S)]] * (PACK - 1) + [[slice(0, HALF), slice(HALF, S)]]
-        for t in range(PACK):
+        both = [keep.tile([P, S], F32, name="both%d" % t) for t in range(PACK)]
+        ratio = [keep.tile([P, S], F32, name="ratio%d" % t) for t in range(PACK)]
+        root = [keep.tile([P, S], F32, name="root%d" % t) for t in range(PACK)]
+        result = [keep.tile([P, S], F32, name="result%d" % t) for t in range(PACK)]
+        whole = slice(0, S)
+
+        def window(t, places, cols):
+            return ex[t][:].indirect(places[:, cols.start // 16 : cols.stop // 16])
+
+        def exp_up(t):
             nc.scalar.activation(out=ex[t][:, :S], in_=h_banks[t][:], func=ACT.Exp, scale=0.5)
-            nc.scalar.activation(out=inv[t][:], in_=h_banks[t][:], func=ACT.Exp, scale=-0.5)
-        for t in range(2, PACK):
-            nc.scalar.activation(out=at_n3[t][:], in_=ex[t][:].indirect(n3_sb[:]), func=ACT.Copy)
-        for t in range(PACK):
-            both = keep.tile([P, S], F32, name="both%d" % t)
-            if t < 2:
-                nc.vector.tensor_copy(out=at_n3[t][:], in_=ex[t][:].indirect(n3_sb[:]))
-            for cols in pieces[t]:
-                nc.vector.tensor_tensor(out=both[:, cols], in0=ex[t][:].indirect(n4_sb[:, cols.start // 16 : cols.stop // 16]),
-                                        in1=at_n3[t][:, cols], op=ALU.add)
-            for cols in pieces[t]:
-                nc.vector.tensor_tensor(out=ratios[t][:, cols], in0=both[:, cols], in1=inv[t][:, cols], op=ALU.mult)
-        for t in range(PACK):
-            root = keep.tile([P, S], F32, name="root%d" % t)
-            result = keep.tile([P, S], F32, name="result%d" % t)
-            for cols in pieces[t]:
-                nc.scalar.activation(out=root[:, cols], in_=ratios[t][:, cols], func=ACT.Abs_reciprocal_sqrt, scale=0.5, bias=0.5)
-                if t < PACK - 1:
-                    nc.scalar.activation(out=result[:, cols], in_=root[:, cols], func=ACT.Square)
-                else:
-                    nc.vector.tensor_tensor(out=result[:, cols], in0=root[:, cols], in1=root[:, cols], op=ALU.mult)
-                nc.sync.dma_start(out=out_rows[t][:, cols], in_=result[:, cols])
+
+        def exp_down(t):
+            nc.scalar.activation(out=inv[t], in_=h_banks[t][:], func=ACT.Exp, scale=-0.5)
+
+        def add_n4(t, cols):
+            nc.vector.tensor_tensor(out=both[t][:, cols], in0=window(t, n4_sb, cols), in1=at_n3[t][:, cols], op=ALU.add)
+
+        def over_ex(t, cols):
+            nc.vector.tensor_tensor(out=ratio[t][:, cols], in0=both[t][:, cols], in1=inv[t][:, cols], op=ALU.mult)
+
+        def inverse_root(t, cols):
+            nc.scalar.activation(out=root[t][:, cols], in_=ratio[t][:, cols], func=ACT.Abs_reciprocal_sqrt, scale=0.5, bias=0.5)
+
+        def square_and_store(t, cols, on_vector):
+            if on_vector:
+                nc.vector.tensor_tensor(out=result[t][:, cols], in0=root[t][:, cols], in1=root[t][:, cols], op=ALU.mult)
+            else:
+                nc.scalar.activation(out=result[t][:, cols], in_=root[t][:, cols], func=ACT.Square)
+            nc.sync.dma_start(out=out_rows[t][:, cols], in_=result[t][:, cols])
+
+        exp_up(0)
+        exp_up(1)
+        exp_down(1)
+        exp_up(2)
+        exp_down(2)
+        exp_down(0)
+        nc.scalar.activation(out=at_n3[2][:], in_=window(2, n3_sb, whole), func=ACT.Copy)
+        exp_up(3)
+        exp_down(3)
+        for cols in halves:
+            nc.vector.tensor_copy(out=at_n3[0][:, cols], in_=window(0, n3_sb, cols))
+        for cols in halves:
+            add_n4(0, cols)
+        nc.vector.tensor_copy(out=at_n3[1][:], in_=window(1, n3_sb, whole))
+        over_ex(0, whole)
+        add_n4(1, whole)
+        nc.scalar.activation(out=at_n3[3][:], in_=window(3, n3_sb, whole), func=ACT.Copy)
+        add_n4(2, whole)
+        over_ex(1, whole)
+        over_ex(2, whole)
+        add_n4(3, halves[0])
+        add_n4(3, halves[1])
+        over_ex(3, halves[0])
+        over_ex(3, halves[1])
+        inverse_root(0, whole)
+        inverse_root(1, whole)
+        square_and_store(0, whole, False)
+        inverse_root(2, whole)
+        square_and_store(1, whole, False)
+        inverse_root(3, halves[0])
+        square_and_store(2, whole, True)
+        inverse_root(3, halves[1])
+        square_and_store(3, halves[0], False)
+        square_and_store(3, halves[1], False)

@@ -73,13 +73,12 @@ def tile_picked_hmixktanhshare_none_p_kernel(tc, x_words, x_scales, w1, gn, w2, 
         xq_scales = place_scales("xq_scales", picked_bytes, nc.sync)
         xq_words = keep.tile([P, S], U32, align_bytes=64)
         nc.vector.tensor_copy(out=xq_words[:], in_=word_table[:].indirect(offs_sb[:]))
-        two_words = keep.tile([P, S], U32, align_bytes=64)
-        nc.vector.tensor_copy(out=two_words[:], in_=word_table[:].indirect(two_sb[:]))
 
         w1_bf = keep.tile([P, PACK * H], BF16, align_bytes=64, tag="w1_bf")
         deal(nc.scalar.copy, w1_bf, w1_raw[0][:], 0, 64)
-        deal(nc.scalar.copy, w1_bf, w1_raw[1][:], 64, 64)
-        w1_codes = keep.tile([P, H], U32, align_bytes=64)
+        deal(nc.scalar.copy, w1_bf, w1_raw[1][:, :, 0:96], 64, 24)
+        deal(nc.vector.tensor_copy, w1_bf, w1_raw[1][:, :, 96:256], 88, 40)
+        w1_codes = keep.tile([P, H], U32, align_bytes=64, tag="w1_codes")
         w1_scales = keep.tile([P, H], U8, align_bytes=64)
         y_banks = []
         for t in range(PACK):
@@ -92,14 +91,16 @@ def tile_picked_hmixktanhshare_none_p_kernel(tc, x_words, x_scales, w1, gn, w2, 
                                 rhs=xq_words[:].bitcast(FP8X4), rhs_scale=xq_scales[:], start=True, stop=True)
             y_banks.append(bank)
 
+        two_words = keep.tile([P, S], U32, align_bytes=64, name="two_words", tag="w1_bf")
+        nc.vector.tensor_copy(out=two_words[:], in_=word_table[:].indirect(two_sb[:]))
         w3_raw = load_weight(w3)
         two_bytes = keep.tile([P, S], U8, align_bytes=64)
         nc.vector.tensor_copy(out=two_bytes[:], in_=byte_table[:].indirect(two_sb[:]))
         gain = keep.tile([P, PACK], F32)
         nc.gpsimd.dma_start(out=gain[:], in_=gn.rearrange("(p t) o -> p (t o)", t=PACK))
-        w2_raw = keep.tile([P, PACK, N], F32, align_bytes=64, name="w2_raw", tag="w1_bf")
+        w2_raw = keep.tile([P, PACK, N], F32, align_bytes=64, name="w2_raw", tag="w1_codes")
         nc.sync.dma_start(out=w2_raw[:], in_=w2.rearrange("(p j) c -> p j c", j=PACK))
-        two_scales = place_scales("two_scales", two_bytes, nc.gpsimd)
+        two_scales = place_scales("two_scales", two_bytes, nc.sync)
 
         z_planes = keep.tile([P, PACK, S], BF16, align_bytes=64, tag="z_planes")
         y_sb = [keep.tile([P, S if t == 2 else 2 * W], F32, name="y_sb%d" % t) for t in range(PACK)]
@@ -141,41 +142,41 @@ def tile_picked_hmixktanhshare_none_p_kernel(tc, x_words, x_scales, w1, gn, w2, 
         fetch_pa(1)
         leave_bank(2)
         tanh_pa(1)
+        fetch_pa(2)
+        leave_bank(3)
+        tanh_pa(2)
         fetch_old(1)
         w3_bf = keep.tile([P, PACK * N], BF16, align_bytes=64, name="w3_bf", tag="pa0")
         deal(nc.vector.tensor_copy, w3_bf, w3_raw[0][:], 0, 64)
         gain_plane(0, slice(0, S))
         deal(nc.vector.tensor_copy, w3_bf, w3_raw[1][:], 64, 64)
-        scatter_sum(1)
+        nc.vector.tensor_tensor(out=old[2][:], in0=y_sb[2][:].indirect(n1_sb[:]), in1=minus_tanh[2][:], op=ALU.add)
         nc.vector.quantize_mx(out=w3_codes[:].bitcast(FP8X4), scales=w3_scales[:], in_=w3_bf[:])
-        fetch_pa(2)
-        leave_bank(3)
-        tanh_pa(2)
+        scatter_sum(1)
         fetch_pa(3)
         fetch_old(3)
         tanh_pa(3)
-        nc.vector.tensor_tensor(out=old[2][:], in0=y_sb[2][:].indirect(n1_sb[:]), in1=minus_tanh[2][:], op=ALU.add)
-        gain_plane(1, slice(0, S))
-        w2_bf = keep.tile([P, PACK * N], BF16, align_bytes=64, name="w2_bf", tag="pa2")
-        deal(nc.scalar.copy, w2_bf, w2_raw[:, :, 0:384], 0, 96)
-        deal(nc.vector.tensor_copy, w2_bf, w2_raw[:, :, 384:N], 96, 32)
-        scatter_sum(3)
         nc.scalar.activation(out=y_sb[2][:].indirect(n1_sb[:]), in_=old[2][:], func=ACT.Copy)
+        w2_bf = keep.tile([P, PACK * N], BF16, align_bytes=64, name="w2_bf", tag="pa3")
+        deal(nc.scalar.copy, w2_bf, w2_raw[:, :, :HALF], 0, 64)
+        nc.scalar.activation(out=z_planes[:, 2, :], in_=y_sb[2][:], func=ACT.Copy, scale=gain[:, 2:3])
+        deal(nc.scalar.copy, w2_bf, w2_raw[:, :, HALF:], 64, 64)
+        gain_plane(1, slice(0, S))
+        scatter_sum(3)
 
         def quantize_w2(t, codes):
             nc.vector.quantize_mx(out=codes.bitcast(FP8X4), scales=w2_scales[:, t * P : (t + 1) * P],
                                   in_=w2_bf[:, t * PACK * P : (t + 1) * PACK * P])
 
-        quantize_w2(0, first_codes[:])
-        gain_plane(3, slice(0, S))
-        nc.scalar.activation(out=z_planes[:, 2, :], in_=y_sb[2][:], func=ACT.Copy, scale=gain[:, 2:3])
+        gain_plane(3, slice(HALF, S))
+        gain_plane(3, slice(0, HALF))
 
         z_bf = keep.tile([P, S * PACK], BF16, align_bytes=64)
         z_to = z_bf[:].rearrange("p (c i t) -> p c t i", i=4, t=PACK)
         z_from = z_planes[:].rearrange("p t (c i) -> p c t i", i=4)
-        nc.scalar.copy(out=z_to[:, 80:128], in_=z_from[:, 80:128])
+        nc.scalar.copy(out=z_to[:, 64:128], in_=z_from[:, 64:128])
         nc.vector.tensor_copy(out=z_to[:, 0:64], in_=z_from[:, 0:64])
-        nc.vector.tensor_copy(out=z_to[:, 64:80], in_=z_from[:, 64:80])
+        quantize_w2(0, first_codes[:])
         z_codes = keep.tile([P, S], U32, align_bytes=64)
         z_scales = keep.tile([P, S], U8, align_bytes=64)
 

from contextlib import ExitStack

import concourse.mybir as mybir

K, T, S, N, H, W = 512, 2048, 512, 512, 512, 384
FLOPS = 2 * K * H * S + 2 * H * N * S + 2 * K * N * S

F32 = mybir.dt.float32
BF16 = mybir.dt.bfloat16
I32 = mybir.dt.int32
U32 = mybir.dt.uint32
U16 = mybir.dt.uint16
U8 = mybir.dt.uint8
FP8X4 = mybir.dt.float8_e4m3fn_x4
ACT = mybir.ActivationFunctionType
ALU = mybir.AluOpType

P = 128
PACK = 4
HALF = S // 2


def deal(engine_copy, dealt, raw, first, count):
    engine_copy(
        out=dealt[:].rearrange("p (t m j) -> p m j t", t=PACK, j=PACK)[:, first : first + count],
        in_=raw.rearrange("p j (m t) -> p m j t", t=PACK),
    )


def tile_picked_hmixktanhshare_none_p_kernel(tc, x_words, x_scales, w1, gn, w2, w3, offs, n1, n2, two, n3, n4, out):
    nc = tc.nc
    with ExitStack() as ctx:
        keep = ctx.enter_context(tc.tile_pool(name="keep", bufs=1))
        psum = ctx.enter_context(tc.psum_pool(name="psum", bufs=1))

        def load_list(name, src):
            tile = keep.tile([P, src.shape[1]], U16, name=name)
            nc.sync.dma_start(out=tile[:], in_=src)
            return tile

        byte_table = keep.tile([P, T], U8, align_bytes=64)
        rows = x_scales[0].bitcast(I32)

        offs_sb = load_list("offs_sb", offs)
        nc.sync.dma_start(out=byte_table[:].bitcast(I32), in_=rows.unsqueeze(1).to_broadcast([16, 8, T // 4]))
        two_sb = load_list("two_sb", two)
        word_table = keep.tile([P, T], U32, align_bytes=64)
        nc.sync.dma_start(out=word_table[:].bitcast(I32), in_=x_words[0].rearrange("p n t -> p (n t)").bitcast(I32))

        def load_weight(w):
            halves = []
            for half in range(2):
                raw = keep.tile([P, PACK, H // 2], F32, name="raw%d" % half, tag="raw%d" % half)
                nc.sync.dma_start(out=raw[:], in_=w.rearrange("(p j) c -> p j c", j=PACK)[:, :, half * (H // 2) : (half + 1) * (H // 2)])
                halves.append(raw)
            return halves

        def place_scales(name, picked, queue):
            plane = keep.tile([P, S], U8, align_bytes=64, name=name)
            nc.vector.tensor_copy(out=plane[:].bitcast(I32), in_=picked[:].bitcast(I32))
            for r in range(1, 4):
                queue.dma_start(out=plane[:].bitcast(I32)[r:P:32, :], in_=picked[:].bitcast(I32)[8 * r : P : 32, :])
            return plane

        w1_raw = load_weight(w1)
        n2_sb = load_list("n2_sb", n2)
        n1_sb = load_list("n1_sb", n1)
        n3_sb = load_list("n3_sb", n3)
        n4_sb = load_list("n4_sb", n4)

        picked_bytes = keep.tile([P, S], U8, align_bytes=64)
        nc.vector.tensor_copy(out=picked_bytes[:], in_=byte_table[:].indirect(offs_sb[:]))
        xq_scales = place_scales("xq_scales", picked_bytes, nc.sync)
        xq_words = keep.tile([P, S], U32, align_bytes=64)
        nc.vector.tensor_copy(out=xq_words[:], in_=word_table[:].indirect(offs_sb[:]))

        w1_bf = keep.tile([P, PACK * H], BF16, align_bytes=64, tag="w1_bf")
        deal(nc.scalar.copy, w1_bf, w1_raw[0][:], 0, 64)
        deal(nc.scalar.copy, w1_bf, w1_raw[1][:, :, 0:96], 64, 24)
        deal(nc.vector.tensor_copy, w1_bf, w1_raw[1][:, :, 96:256], 88, 40)
        w1_codes = keep.tile([P, H], U32, align_bytes=64, tag="w1_codes")
        w1_scales = keep.tile([P, H], U8, align_bytes=64)
        y_banks = []
        for t in range(PACK):
            cols = slice(t * P, (t + 1) * P)
            nc.vector.quantize_mx(out=w1_codes[:, cols].bitcast(FP8X4), scales=w1_scales[:, cols], in_=w1_bf[:, t * PACK * P : (t + 1) * PACK * P])
        for t in range(PACK):
            cols = slice(t * P, (t + 1) * P)
            bank = psum.tile([P, S], F32, name="y_bank%d" % t)
            nc.tensor.matmul_mx(out=bank[:], lhsT=w1_codes[:, cols].bitcast(FP8X4), lhsT_scale=w1_scales[:, cols],
                                rhs=xq_words[:].bitcast(FP8X4), rhs_scale=xq_scales[:], start=True, stop=True)
            y_banks.append(bank)

        two_words = keep.tile([P, S], U32, align_bytes=64, name="two_words", tag="w1_bf")
        nc.vector.tensor_copy(out=two_words[:], in_=word_table[:].indirect(two_sb[:]))
        w3_raw = load_weight(w3)
        two_bytes = keep.tile([P, S], U8, align_bytes=64)
        nc.vector.tensor_copy(out=two_bytes[:], in_=byte_table[:].indirect(two_sb[:]))
        gain = keep.tile([P, PACK], F32)
        nc.gpsimd.dma_start(out=gain[:], in_=gn.rearrange("(p t) o -> p (t o)", t=PACK))
        w2_raw = keep.tile([P, PACK, N], F32, align_bytes=64, name="w2_raw", tag="w1_codes")
        nc.sync.dma_start(out=w2_raw[:], in_=w2.rearrange("(p j) c -> p j c", j=PACK))
        two_scales = place_scales("two_scales", two_bytes, nc.sync)

        z_planes = keep.tile([P, PACK, S], BF16, align_bytes=64, tag="z_planes")
        y_sb = [keep.tile([P, S if t == 2 else 2 * W], F32, name="y_sb%d" % t) for t in range(PACK)]
        pa = [keep.tile([P, W], F32, name="pa%d" % t, tag="pa%d" % t, align_bytes=64) for t in range(PACK)]
        minus_tanh = [keep.tile([P, W], F32, name="minus_tanh%d" % t) for t in range(PACK)]
        old = [keep.tile([P, W], F32, name="old%d" % t, tag="old%d" % t, align_bytes=64) for t in range(PACK)]
        for t in (0, 1, 3):
            nc.gpsimd.memset(y_sb[t][:, S:], 0.0)

        def leave_bank(t):
            nc.scalar.copy(out=y_sb[t][:, :S], in_=y_banks[t][:])

        def fetch_pa(t):
            nc.scalar.activation(out=pa[t][:], in_=y_sb[t][:].indirect(n2_sb[:]), func=ACT.Copy)

        def tanh_pa(t):
            nc.scalar.activation(out=minus_tanh[t][:], in_=pa[t][:], func=ACT.Tanh, scale=-1.0)

        def fetch_old(t):
            nc.scalar.activation(out=old[t][:], in_=y_sb[t][:].indirect(n1_sb[:]), func=ACT.Copy)

        def scatter_sum(t):
            nc.vector.tensor_tensor(out=y_sb[t][:].indirect(n1_sb[:]), in0=old[t][:], in1=minus_tanh[t][:], op=ALU.add)

        def gain_plane(t, cols):
            nc.vector.tensor_scalar(out=z_planes[:, t, cols], in0=y_sb[t][:, cols], scalar1=gain[:, t : t + 1], scalar2=None, op0=ALU.mult)

        w3_codes = keep.tile([P, N], U32, align_bytes=64)
        w3_scales = keep.tile([P, N], U8, align_bytes=64)
        first_codes = keep.tile([P, P], U32, align_bytes=64)
        w2_scales = keep.tile([P, N], U8, align_bytes=64)

        leave_bank(0)
        nc.vector.tensor_copy(out=y_sb[1][:, :S], in_=y_banks[1][:])
        fetch_pa(0)
        tanh_pa(0)
        nc.vector.tensor_copy(out=old[0][:], in_=y_sb[0][:].indirect(n1_sb[:]))
        scatter_sum(0)
        fetch_pa(1)
        leave_bank(2)
        tanh_pa(1)
        fetch_pa(2)
        leave_bank(3)
        tanh_pa(2)
        fetch_old(1)
        w3_bf = keep.tile([P, PACK * N], BF16, align_bytes=64, name="w3_bf", tag="pa0")
        deal(nc.vector.tensor_copy, w3_bf, w3_raw[0][:], 0, 64)
        gain_plane(0, slice(0, S))
        deal(nc.vector.tensor_copy, w3_bf, w3_raw[1][:], 64, 64)
        nc.vector.tensor_tensor(out=old[2][:], in0=y_sb[2][:].indirect(n1_sb[:]), in1=minus_tanh[2][:], op=ALU.add)
        nc.vector.quantize_mx(out=w3_codes[:].bitcast(FP8X4), scales=w3_scales[:], in_=w3_bf[:])
        scatter_sum(1)
        fetch_pa(3)
        fetch_old(3)
        tanh_pa(3)
        nc.scalar.activation(out=y_sb[2][:].indirect(n1_sb[:]), in_=old[2][:], func=ACT.Copy)
        w2_bf = keep.tile([P, PACK * N], BF16, align_bytes=64, name="w2_bf", tag="pa3")
        deal(nc.scalar.copy, w2_bf, w2_raw[:, :, :HALF], 0, 64)
        nc.scalar.activation(out=z_planes[:, 2, :], in_=y_sb[2][:], func=ACT.Copy, scale=gain[:, 2:3])
        deal(nc.scalar.copy, w2_bf, w2_raw[:, :, HALF:], 64, 64)
        gain_plane(1, slice(0, S))
        scatter_sum(3)

        def quantize_w2(t, codes):
            nc.vector.quantize_mx(out=codes.bitcast(FP8X4), scales=w2_scales[:, t * P : (t + 1) * P],
                                  in_=w2_bf[:, t * PACK * P : (t + 1) * PACK * P])

        gain_plane(3, slice(HALF, S))
        gain_plane(3, slice(0, HALF))

        z_bf = keep.tile([P, S * PACK], BF16, align_bytes=64)
        z_to = z_bf[:].rearrange("p (c i t) -> p c t i", i=4, t=PACK)
        z_from = z_planes[:].rearrange("p t (c i) -> p c t i", i=4)
        nc.scalar.copy(out=z_to[:, 64:128], in_=z_from[:, 64:128])
        nc.vector.tensor_copy(out=z_to[:, 0:64], in_=z_from[:, 0:64])
        quantize_w2(0, first_codes[:])
        z_codes = keep.tile([P, S], U32, align_bytes=64)
        z_scales = keep.tile([P, S], U8, align_bytes=64)

        def quantize_z(half):
            cols = slice(half * HALF, (half + 1) * HALF)
            nc.vector.quantize_mx(out=z_codes[:, cols].bitcast(FP8X4), scales=z_scales[:, cols],
                                  in_=z_bf[:, half * HALF * PACK : (half + 1) * HALF * PACK])

        quantize_z(0)
        quantize_z(1)
        later_codes = keep.tile([P, PACK - 1, P], U32, align_bytes=64, tag="z_planes")
        for t in range(1, PACK):
            quantize_w2(t, later_codes[:, t - 1, :])

        h_banks = []
        for t in range(PACK):
            cols = slice(t * P, (t + 1) * P)
            bank = psum.tile([P, S], F32, name="h_bank%d" % t)
            nc.tensor.matmul_mx(out=bank[:], lhsT=w3_codes[:, cols].bitcast(FP8X4), lhsT_scale=w3_scales[:, cols],
                                rhs=two_words[:].bitcast(FP8X4), rhs_scale=two_scales[:], start=True, stop=False)
            h_banks.append(bank)
        for t in range(PACK):
            cols = slice(t * P, (t + 1) * P)
            codes = first_codes[:] if t == 0 else later_codes[:, t - 1, :]
            for places in [slice(0, HALF), slice(HALF, S)] if t == 0 else [slice(0, S)]:
                nc.tensor.matmul_mx(out=h_banks[t][:, places], lhsT=codes.bitcast(FP8X4), lhsT_scale=w2_scales[:, cols],
                                    rhs=z_codes[:, places].bitcast(FP8X4), rhs_scale=z_scales[:, places], start=False, stop=(places.stop == S))

        out_rows = out.rearrange("(p t) n -> t p n", t=PACK)
        halves = [slice(0, HALF), slice(HALF, S)]
        ex = [keep.tile([P, S if t == 0 else 2 * S], F32, name="ex%d" % t) for t in range(PACK)]
        inv0 = keep.tile([P, S], F32)
        inv = [inv0[:]] + [ex[t][:, S:] for t in range(1, PACK)]
        at_n3 = [keep.tile([P, S], F32, name="at_n3_%d" % t) for t in range(PACK)]
        both = [keep.tile([P, S], F32, name="both%d" % t) for t in range(PACK)]
        ratio = [keep.tile([P, S], F32, name="ratio%d" % t) for t in range(PACK)]
        root = [keep.tile([P, S], F32, name="root%d" % t) for t in range(PACK)]
        result = [keep.tile([P, S], F32, name="result%d" % t) for t in range(PACK)]
        whole = slice(0, S)

        def window(t, places, cols):
            return ex[t][:].indirect(places[:, cols.start // 16 : cols.stop // 16])

        def exp_up(t):
            nc.scalar.activation(out=ex[t][:, :S], in_=h_banks[t][:], func=ACT.Exp, scale=0.5)

        def exp_down(t):
            nc.scalar.activation(out=inv[t], in_=h_banks[t][:], func=ACT.Exp, scale=-0.5)

        def add_n4(t, cols):
            nc.vector.tensor_tensor(out=both[t][:, cols], in0=window(t, n4_sb, cols), in1=at_n3[t][:, cols], op=ALU.add)

        def over_ex(t, cols):
            nc.vector.tensor_tensor(out=ratio[t][:, cols], in0=both[t][:, cols], in1=inv[t][:, cols], op=ALU.mult)

        def inverse_root(t, cols):
            nc.scalar.activation(out=root[t][:, cols], in_=ratio[t][:, cols], func=ACT.Abs_reciprocal_sqrt, scale=0.5, bias=0.5)

        def square_and_store(t, cols, on_vector):
            if on_vector:
                nc.vector.tensor_tensor(out=result[t][:, cols], in0=root[t][:, cols], in1=root[t][:, cols], op=ALU.mult)
            else:
                nc.scalar.activation(out=result[t][:, cols], in_=root[t][:, cols], func=ACT.Square)
            nc.sync.dma_start(out=out_rows[t][:, cols], in_=result[t][:, cols])

        exp_up(0)
        exp_up(1)
        exp_down(1)
        exp_up(2)
        exp_down(2)
        exp_down(0)
        nc.scalar.activation(out=at_n3[2][:], in_=window(2, n3_sb, whole), func=ACT.Copy)
        exp_up(3)
        exp_down(3)
        for cols in halves:
            nc.vector.tensor_copy(out=at_n3[0][:, cols], in_=window(0, n3_sb, cols))
        for cols in halves:
            add_n4(0, cols)
        nc.vector.tensor_copy(out=at_n3[1][:], in_=window(1, n3_sb, whole))
        over_ex(0, whole)
        add_n4(1, whole)
        nc.scalar.activation(out=at_n3[3][:], in_=window(3, n3_sb, whole), func=ACT.Copy)
        add_n4(2, whole)
        over_ex(1, whole)
        over_ex(2, whole)
        add_n4(3, halves[0])
        add_n4(3, halves[1])
        over_ex(3, halves[0])
        over_ex(3, halves[1])
        inverse_root(0, whole)
        inverse_root(1, whole)
        square_and_store(0, whole, False)
        inverse_root(2, whole)
        square_and_store(1, whole, False)
        inverse_root(3, halves[0])
        square_and_store(2, whole, True)
        inverse_root(3, halves[1])
        square_and_store(3, halves[0], False)
        square_and_store(3, halves[1], False)
